import numpy as np
import ml_dtypes


def mxq(x, axis, fmt="e4m3"):
    dtype, down = {"e4m3": (ml_dtypes.float8_e4m3fn, 7), "e5m2": (ml_dtypes.float8_e5m2, 14)}[fmt]
    v = np.moveaxis(np.asarray(x, np.float32).astype(ml_dtypes.bfloat16).astype(np.float64), axis, -1)
    blocks = v.reshape(v.shape[:-1] + (-1, 32))
    amax = np.abs(blocks).max(-1, keepdims=True)
    byte = np.maximum(np.where(amax > 0, np.frexp(amax)[1] - 1 + 127, 0) - down, 1)
    scale = np.exp2(byte - 127.0)
    codes = (blocks / scale).astype(np.float32).astype(dtype).astype(np.float64)
    return np.moveaxis((codes * scale).reshape(v.shape), -1, axis)


WIDE = False


def mx_kscale(k):
    if not WIDE:
        return np.ones(k)
    levels = np.array([10, -10, 5, -5, 0])
    if k % 512:
        return np.exp2(np.random.permutation(np.resize(levels, k // 32))).repeat(32)
    a = np.empty((k // 512, 16))
    for p in range(k // 512):
        a[p, :8] = np.random.permutation(np.resize(levels, 8))
        for g in range(8):
            far = levels[np.abs(levels - a[p, g]) >= 10]
            a[p, g + 8] = far[np.random.randint(len(far))]
    return np.exp2(a.ravel()).repeat(32)


def f64(x):
    return np.asarray(x).astype(np.float64)


def striped(idx):
    return np.tile(idx.reshape(-1, 16).T, (8, 1)).astype(np.uint16)


def unstriped(offs):
    return offs[:16].T.reshape(-1).astype(np.int64)


def silu(v):
    return v / (1.0 + np.exp(-np.maximum(v, -700.0)))

def planes(y):
    n, m = y.shape
    v = y.astype(np.float32).astype(ml_dtypes.bfloat16).astype(np.float64).reshape(n // 32, 32, m)
    top = np.abs(v).max(1)
    byte = np.clip(np.where(top > 0, np.frexp(top)[1] - 1 + 127 - 7, 1), 1, 254)
    codes = (v * np.exp2(127.0 - byte)[:, None, :]).reshape(n, m).astype(np.float32).astype(ml_dtypes.float8_e4m3fn).view(np.uint8)
    words = codes.reshape(n // 512, 128, 4, m).transpose(0, 1, 3, 2)
    return np.ascontiguousarray(words), np.ascontiguousarray(byte.astype(np.uint8).reshape(n // 512, 16, m))


K, T, S, V, H, J, U = 512, 2048, 512, 256, 512, 512, 512


def setup_inputs():
    n = np.random.standard_normal
    s = mx_kscale(K)[:, None]
    u = mx_kscale(H)
    r = mx_kscale(J)[:, None]
    return {
        "xT": (n((K, T)) * s).astype(np.float32),
        "aT": (n((J, U)) * r).astype(np.float32),
        "w1": (n((K, H)) / np.sqrt(K) / s * u).astype(np.float32),
        "w3": (n((J, H)) / np.sqrt(J) / r).astype(np.float32),
        "w2": (n((H, H)) / np.sqrt(2 * H) / u[:, None]).astype(np.float32),
        "offs": striped(np.random.permutation(T)[:S]),
        "pos1": striped(np.random.permutation(S)[:V]),
        "pos2": striped(np.random.permutation(S)[:V]),
    }


def reference(xT, aT, w1, w3, w2, offs, pos1, pos2):
    xq = mxq(f64(xT)[:, unstriped(offs)], 0, "e4m3")
    h = silu(mxq(f64(w1), 0, "e4m3").T @ xq)
    f = mxq(f64(w3), 0, "e4m3").T @ mxq(f64(aT), 0, "e4m3")
    z = h[:, unstriped(pos1)] * f[:, :V] + h[:, unstriped(pos2)] * f[:, V:2 * V]
    out_0 = mxq(f64(w2), 0, "e4m3").T @ mxq(z, 0, "e4m3")
    return (out_0,) + planes(out_0)

@@ -1,0 +1,221 @@
+from contextlib import ExitStack
+
+import concourse.mybir as mybir
+
+K, T, S, V, H = 512, 2048, 512, 256, 512
+FLOPS = 2 * (K * H * S + K * H * 2 * V + H * H * V)
+
+F32 = mybir.dt.float32
+BF16 = mybir.dt.bfloat16
+I32 = mybir.dt.int32
+U32 = mybir.dt.uint32
+U16 = mybir.dt.uint16
+U8 = mybir.dt.uint8
+FP8X4 = mybir.dt.float8_e4m3fn_x4
+ACT = mybir.ActivationFunctionType
+ALU = mybir.AluOpType
+
+P = 128
+PACK = 4
+HALF = 256
+VH = 128
+
+
+def tile_picked_dime_none_lo_kernel(
+    tc, xT, aT, w1, w3, w2, offs, pos1, pos2, out_0, out_1, out_2
+):
+    nc = tc.nc
+    with ExitStack() as ctx:
+        lists = ctx.enter_context(tc.tile_pool(name="lists", bufs=1))
+        sb = ctx.enter_context(tc.tile_pool(name="sb", bufs=1))
+        psum = ctx.enter_context(tc.psum_pool(name="psum", bufs=1))
+
+        def by_rows(dram):
+            return dram.rearrange("(p j) c -> p j c", j=PACK)
+
+        def load_half(dram, half, name, tag=None):
+            raw = sb.tile([P, PACK, HALF], F32, name=name, tag=tag or name, align_bytes=64)
+            nc.sync.dma_start(out=raw[:], in_=by_rows(dram)[:, :, half * HALF : (half + 1) * HALF])
+            return raw
+
+        def mx_tiles(width, name):
+            codes = sb.tile([P, width], U32, name=name + "_codes", align_bytes=64)
+            scales = sb.tile([P, width], U8, name=name + "_scales", align_bytes=64)
+            return codes, scales
+
+        def quantize(mx, rounded, cols=None):
+            codes, scales = mx
+            cols = slice(None) if cols is None else cols
+            nc.vector.quantize_mx(out=codes[:, cols].bitcast(FP8X4), scales=scales[:, cols], in_=rounded)
+
+        def product(out, weights, t, moving):
+            cols = slice(t * P, (t + 1) * P)
+            nc.tensor.matmul_mx(
+                out=out,
+                lhsT=weights[0][:, cols].bitcast(FP8X4),
+                lhsT_scale=weights[1][:, cols],
+                rhs=moving[0][:].bitcast(FP8X4),
+                rhs_scale=moving[1][:],
+                start=True,
+                stop=True,
+            )
+
+        def deal(copy, rounded, raw, m0):
+            count = raw.shape[2] // PACK
+            copy(
+                out=rounded[:].rearrange("p (t m j) -> p m j t", t=PACK, j=PACK)[:, m0 : m0 + count],
+                in_=raw[:].rearrange("p j (m t) -> p m j t", t=PACK),
+            )
+
+        def woven(ap):
+            return ap.rearrange("p (c i j) -> p c j i", i=4, j=PACK)
+
+        def planar(ap):
+            return ap.rearrange("p j (c i) -> p c j i", i=4)
+
+        offs_sb = lists.tile([P, S // 16], U16, name="offs_sb")
+        pos_sb = [lists.tile([P, V // 16], U16, name=f"pos{d}_sb") for d in range(2)]
+
+        x_raw = [sb.tile([P, T], F32, name=f"x_raw{j}") for j in range(PACK)]
+        nc.sync.dma_start(out=x_raw[0][:], in_=by_rows(xT)[:, 0, :])
+        nc.sync.dma_start(offs_sb[:], offs)
+        for j in range(1, PACK):
+            nc.sync.dma_start(out=x_raw[j][:], in_=by_rows(xT)[:, j, :])
+        w1_raw = [load_half(w1, half, f"w1_raw{half}") for half in range(2)]
+        nc.sync.dma_start(pos_sb[0][:], pos1)
+        nc.sync.dma_start(pos_sb[1][:], pos2)
+        a_raw = [load_half(aT, 0, "a_raw0", "first")]
+        w3_raw = [load_half(w3, 0, "w3_raw0"), load_half(w3, 1, "w3_raw1", "chain")]
+        a_raw.append(load_half(aT, 1, "a_raw1", "second"))
+        w2_raw = sb.tile([P, PACK, H], F32, name="w2_raw")
+        nc.sync.dma_start(out=w2_raw[:], in_=by_rows(w2))
+
+        x_bf = sb.tile([P, S, PACK], BF16, name="x_bf", align_bytes=64)
+        for j in range(PACK):
+            nc.vector.tensor_copy(out=x_bf[:, :, j], in_=x_raw[j][:].indirect(offs_sb[:]))
+        x_mx = mx_tiles(S, "x")
+        quantize(x_mx, x_bf[:].rearrange("p s j -> p (s j)"))
+
+        w1_bf = sb.tile([P, PACK * H], BF16, name="w1_bf", align_bytes=64)
+        deal(nc.scalar.copy, w1_bf, w1_raw[0], 0)
+        deal(nc.vector.tensor_copy, w1_bf, w1_raw[1], HALF // PACK)
+        w1_mx = mx_tiles(H, "w1")
+        quantize(w1_mx, w1_bf[:])
+
+        h_bank = [psum.tile([P, S], F32, name=f"h_bank{t}", tag=f"bank{t}") for t in range(PACK)]
+        for t in range(PACK):
+            product(h_bank[t][:], w1_mx, t, x_mx)
+
+        w3_bf = sb.tile([P, PACK * H], BF16, name="w3_bf", align_bytes=64)
+        a_bf = [sb.tile([P, PACK * V], BF16, name="a_bf0", align_bytes=64)]
+        w3_mx = mx_tiles(H, "w3")
+        a_mx = [mx_tiles(V, f"a{d}") for d in range(2)]
+        f_bank = [
+            [psum.tile([P, 2, V], F32, name=f"f_bank{d}{pair}", tag=f"bank{4 + 2 * d + pair}") for pair in range(2)]
+            for d in range(2)
+        ]
+        picked = [[sb.tile([P, 2, V], F32, name=f"picked{d}{pair}") for pair in range(2)] for d in range(2)]
+        term = []
+        w2_mx = mx_tiles(H, "w2")
+
+        def fetch_args(h, d, t):
+            return {"out": picked[d][t // 2][:, t % 2, :], "in_": h[:, t, :].indirect(pos_sb[d][:])}
+
+        def filters(d):
+            for t in range(PACK):
+                product(f_bank[d][t // 2][:, t % 2, :], w3_mx, t, a_mx[d])
+
+        def weigh(d, pair, cols=slice(0, V)):
+            nc.vector.tensor_tensor(
+                out=term[d][:, 2 * pair : 2 * pair + 2, cols],
+                in0=picked[d][pair][:, :, cols],
+                in1=f_bank[d][pair][:, :, cols],
+                op=ALU.mult,
+            )
+
+        nc.scalar.copy(out=woven(a_bf[0][:]), in_=planar(a_raw[0][:]))
+        h = sb.tile([P, PACK, S], F32, name="h", tag="first", align_bytes=64)
+        for t in range(PACK):
+            nc.scalar.activation(out=h[:, t, :], in_=h_bank[t][:], func=ACT.Silu)
+        for d, t in [(d, t) for d in range(2) for t in range(PACK)]:
+            nc.scalar.activation(func=ACT.Copy, **fetch_args(h, d, t))
+
+        deal(nc.vector.tensor_copy, w3_bf, w3_raw[0], 0)
+        quantize(a_mx[0], a_bf[0][:])
+        deal(nc.vector.tensor_copy, w3_bf, w3_raw[1], HALF // PACK)
+        quantize(w3_mx, w3_bf[:])
+        filters(0)
+        a_bf.append(sb.tile([P, PACK * V], BF16, name="a_bf1", tag="chain", align_bytes=64))
+        nc.vector.tensor_copy(out=woven(a_bf[1][:]), in_=planar(a_raw[1][:]))
+        term.append(sb.tile([P, PACK, V], F32, name="term0", tag="second", align_bytes=64))
+        quantize(a_mx[1], a_bf[1][:])
+        filters(1)
+        weigh(0, 0)
+        w2_bf = sb.tile([P, PACK * H], BF16, name="w2_bf", tag="chain", align_bytes=64)
+        deal(nc.vector.tensor_copy, w2_bf, w2_raw, 0)
+        weigh(0, 1)
+        quantize(w2_mx, w2_bf[:])
+        term.append(sb.tile([P, PACK, V], F32, name="term1", tag="chain", align_bytes=64))
+        z_bf = [sb.tile([P, PACK * VH], BF16, name=f"z_bf{part}", align_bytes=64) for part in range(2)]
+        z_mx = [mx_tiles(VH, f"z{part}") for part in range(2)]
+        part_cols = [slice(part * VH, (part + 1) * VH) for part in range(2)]
+
+        def add_terms(part):
+            cols = part_cols[part]
+            nc.vector.tensor_tensor(
+                out=woven(z_bf[part][:]), in0=planar(term[0][:, :, cols]), in1=planar(term[1][:, :, cols]), op=ALU.add
+            )
+
+        y_bank = [
+            [psum.tile([P, 2, VH], F32, name=f"y_bank{part}{pair}", tag=f"bank{2 * part + pair}") for pair in range(2)]
+            for part in range(2)
+        ]
+        y = [sb.tile([P, PACK, VH], F32, name=f"y{part}") for part in range(2)]
+        y_bf = [sb.tile([P, PACK * VH], BF16, name=f"y_bf{part}", align_bytes=64) for part in range(2)]
+        y_mx = mx_tiles(V, "y")
+
+        def project(part):
+            for t in range(PACK):
+                product(y_bank[part][t // 2][:, t % 2, :], w2_mx, t, z_mx[part])
+
+        def keep(part, pair):
+            nc.scalar.copy(out=y[part][:, 2 * pair : 2 * pair + 2, :], in_=y_bank[part][pair][:])
+
+        def round_pair(part, pair):
+            nc.vector.tensor_copy(
+                out=y_bf[part][:].rearrange("p (c j) -> p c j", j=PACK)[:, :, 2 * pair : 2 * pair + 2],
+                in_=y_bank[part][pair][:].rearrange("p j c -> p c j"),
+            )
+
+        def store_y(part):
+            nc.sync.dma_start(out=by_rows(out_0)[:, :, part_cols[part]], in_=y[part][:])
+
+        weigh(1, 0, part_cols[0])
+        weigh(1, 1, part_cols[0])
+        weigh(1, 0, part_cols[1])
+        add_terms(0)
+        weigh(1, 1, part_cols[1])
+        quantize(z_mx[0], z_bf[0][:])
+        project(0)
+        add_terms(1)
+        quantize(z_mx[1], z_bf[1][:])
+        project(1)
+
+        keep(0, 0)
+        keep(0, 1)
+        store_y(0)
+        nc.vector.tensor_copy(out=woven(y_bf[0][:]), in_=planar(y[0][:]))
+        round_pair(1, 0)
+        keep(1, 1)
+        keep(1, 0)
+        store_y(1)
+        quantize(y_mx, y_bf[0][:], part_cols[0])
+        round_pair(1, 1)
+        quantize(y_mx, y_bf[1][:], part_cols[1])
+
+        nc.sync.dma_start(out=out_1[0].rearrange("p c r -> p (c r)").bitcast(I32), in_=y_mx[0][:].bitcast(I32))
+        for q in range(4):
+            queue = nc.scalar if q % 2 else nc.sync
+            queue.dma_start(
+                out=out_2[0][4 * q : 4 * q + 4, :].bitcast(I32), in_=y_mx[1][32 * q : 32 * q + 4, :].bitcast(I32)
+            )

@@ -90,6 +90,10 @@ def tile_picked_dime_none_lo_kernel(
         w2_raw = sb.tile([P, PACK, H], F32, name="w2_raw")
         nc.sync.dma_start(out=w2_raw[:], in_=by_rows(w2))
 
+        warm = sb.tile([P, 2], F32, name="warm")
+        nc.vector.memset(warm[:, 0:1], 0.0)
+        nc.scalar.activation(out=warm[:, 1:2], in_=warm[:, 0:1], func=ACT.Silu)
+
         x_bf = sb.tile([P, S, PACK], BF16, name="x_bf", align_bytes=64)
         for j in range(PACK):
             nc.vector.tensor_copy(out=x_bf[:, :, j], in_=x_raw[j][:].indirect(offs_sb[:]))

@@ -17,8 +17,8 @@ ALU = mybir.AluOpType
 
 P = 128
 PACK = 4
-HALF = 256
 VH = 128
+W1_SCALAR = 48
 
 
 def tile_picked_dime_none_lo_kernel(
@@ -33,19 +33,18 @@ def tile_picked_dime_none_lo_kernel(
         def by_rows(dram):
             return dram.rearrange("(p j) c -> p j c", j=PACK)
 
-        def load_half(dram, half, name, tag=None):
-            raw = sb.tile([P, PACK, HALF], F32, name=name, tag=tag or name, align_bytes=64)
-            nc.sync.dma_start(out=raw[:], in_=by_rows(dram)[:, :, half * HALF : (half + 1) * HALF])
+        def load(dram, name):
+            raw = sb.tile([P, PACK, H], F32, name=name, tag=name, align_bytes=64)
+            nc.sync.dma_start(out=raw[:], in_=by_rows(dram))
             return raw
 
-        def mx_tiles(width, name):
-            codes = sb.tile([P, width], U32, name=name + "_codes", align_bytes=64)
+        def mx_tiles(width, name, tag=None):
+            codes = sb.tile([P, width], U32, name=name + "_codes", tag=tag or name + "_codes", align_bytes=64)
             scales = sb.tile([P, width], U8, name=name + "_scales", align_bytes=64)
             return codes, scales
 
-        def quantize(mx, rounded, cols=None):
+        def quantize(mx, rounded, cols=slice(None)):
             codes, scales = mx
-            cols = slice(None) if cols is None else cols
             nc.vector.quantize_mx(out=codes[:, cols].bitcast(FP8X4), scales=scales[:, cols], in_=rounded)
 
         def product(out, weights, t, moving):
@@ -60,11 +59,10 @@ def tile_picked_dime_none_lo_kernel(
                 stop=True,
             )
 
-        def deal(copy, rounded, raw, m0):
-            count = raw.shape[2] // PACK
+        def deal(copy, rounded, raw, m0, m1):
             copy(
-                out=rounded[:].rearrange("p (t m j) -> p m j t", t=PACK, j=PACK)[:, m0 : m0 + count],
-                in_=raw[:].rearrange("p j (m t) -> p m j t", t=PACK),
+                out=rounded[:].rearrange("p (t m j) -> p m j t", t=PACK, j=PACK)[:, m0:m1],
+                in_=raw.rearrange("p j (m t) -> p m j t", t=PACK),
             )
 
         def woven(ap):
@@ -81,14 +79,14 @@ def tile_picked_dime_none_lo_kernel(
         nc.sync.dma_start(offs_sb[:], offs)
         for j in range(1, PACK):
             nc.sync.dma_start(out=x_raw[j][:], in_=by_rows(xT)[:, j, :])
-        w1_raw = [load_half(w1, half, f"w1_raw{half}") for half in range(2)]
+        w1_raw = load(w1, "w1_raw")
         nc.sync.dma_start(pos_sb[0][:], pos1)
         nc.sync.dma_start(pos_sb[1][:], pos2)
-        a_raw = [load_half(aT, 0, "a_raw0", "first")]
-        w3_raw = [load_half(w3, 0, "w3_raw0"), load_half(w3, 1, "w3_raw1", "chain")]
-        a_raw.append(load_half(aT, 1, "a_raw1", "second"))
-        w2_raw = sb.tile([P, PACK, H], F32, name="w2_raw")
-        nc.sync.dma_start(out=w2_raw[:], in_=by_rows(w2))
+        w3_raw = load(w3, "w3_raw")
+        a_raw = load(aT, "a_raw")
+        w2_raw = [sb.tile([P, PACK, H // 2], F32, name=f"w2_raw{half}", tag=f"w2_raw{half}") for half in range(2)]
+        for half in range(2):
+            nc.sync.dma_start(out=w2_raw[half][:], in_=by_rows(w2)[:, :, half * H // 2 : (half + 1) * H // 2])
 
         warm = sb.tile([P, 2], F32, name="warm")
         nc.vector.memset(warm[:, 0:1], 0.0)
@@ -101,65 +99,60 @@ def tile_picked_dime_none_lo_kernel(
         quantize(x_mx, x_bf[:].rearrange("p s j -> p (s j)"))
 
         w1_bf = sb.tile([P, PACK * H], BF16, name="w1_bf", align_bytes=64)
-        deal(nc.scalar.copy, w1_bf, w1_raw[0], 0)
-        deal(nc.vector.tensor_copy, w1_bf, w1_raw[1], HALF // PACK)
+        deal(nc.scalar.copy, w1_bf, w1_raw[:, :, : PACK * W1_SCALAR], 0, W1_SCALAR)
+        deal(nc.vector.tensor_copy, w1_bf, w1_raw[:, :, PACK * W1_SCALAR :], W1_SCALAR, P)
         w1_mx = mx_tiles(H, "w1")
-        quantize(w1_mx, w1_bf[:])
+        quantize(w1_mx, w1_bf[:, : PACK * P], slice(0, P))
+        quantize(w1_mx, w1_bf[:, PACK * P :], slice(P, H))
 
         h_bank = [psum.tile([P, S], F32, name=f"h_bank{t}", tag=f"bank{t}") for t in range(PACK)]
+        h = [sb.tile([P, S], F32, name=f"h{t}") for t in range(PACK)]
         for t in range(PACK):
             product(h_bank[t][:], w1_mx, t, x_mx)
+            nc.scalar.activation(out=h[t][:], in_=h_bank[t][:], func=ACT.Silu)
 
         w3_bf = sb.tile([P, PACK * H], BF16, name="w3_bf", align_bytes=64)
-        a_bf = [sb.tile([P, PACK * V], BF16, name="a_bf0", align_bytes=64)]
         w3_mx = mx_tiles(H, "w3")
+        deal(nc.vector.tensor_copy, w3_bf, w3_raw[:], 0, P)
+
+        picked = [
+            [
+                sb.tile([P, 2, V], F32, name=f"picked{d}{pair}", tag=f"picked{d}{pair}", align_bytes=64)
+                for pair in range(2)
+            ]
+            for d in range(2)
+        ]
+
+        def fetch_args(d, t):
+            return {"out": picked[d][t // 2][:, t % 2, :], "in_": h[t][:].indirect(pos_sb[d][:])}
+
+        quantize(w3_mx, w3_bf[:])
+        for d, t in [(d, t) for d in range(2) for t in range(PACK)]:
+            nc.scalar.activation(func=ACT.Copy, **fetch_args(d, t))
+
+        a_bf = [sb.tile([P, PACK * V], BF16, name=f"a_bf{d}", align_bytes=64) for d in range(2)]
         a_mx = [mx_tiles(V, f"a{d}") for d in range(2)]
         f_bank = [
             [psum.tile([P, 2, V], F32, name=f"f_bank{d}{pair}", tag=f"bank{4 + 2 * d + pair}") for pair in range(2)]
             for d in range(2)
         ]
-        picked = [[sb.tile([P, 2, V], F32, name=f"picked{d}{pair}") for pair in range(2)] for d in range(2)]
-        term = []
-        w2_mx = mx_tiles(H, "w2")
-
-        def fetch_args(h, d, t):
-            return {"out": picked[d][t // 2][:, t % 2, :], "in_": h[:, t, :].indirect(pos_sb[d][:])}
-
-        def filters(d):
+        for d in range(2):
+            nc.vector.tensor_copy(out=woven(a_bf[d][:]), in_=planar(a_raw[:, :, d * V : (d + 1) * V]))
+        for d in range(2):
+            quantize(a_mx[d], a_bf[d][:])
             for t in range(PACK):
                 product(f_bank[d][t // 2][:, t % 2, :], w3_mx, t, a_mx[d])
 
-        def weigh(d, pair, cols=slice(0, V)):
+        w2_bf = sb.tile([P, PACK * H], BF16, name="w2_bf", align_bytes=64)
+        deal(nc.vector.tensor_copy, w2_bf, w2_raw[0][:], 0, P // 2)
+        deal(nc.scalar.copy, w2_bf, w2_raw[1][:], P // 2, P)
+        term = [sb.tile([P, PACK, V], F32, name=f"term{d}", tag="term1" if d else "w2_raw0") for d in range(2)]
+
+        def weigh(d, pair):
             nc.vector.tensor_tensor(
-                out=term[d][:, 2 * pair : 2 * pair + 2, cols],
-                in0=picked[d][pair][:, :, cols],
-                in1=f_bank[d][pair][:, :, cols],
-                op=ALU.mult,
+                out=term[d][:, 2 * pair : 2 * pair + 2, :], in0=picked[d][pair][:], in1=f_bank[d][pair][:], op=ALU.mult
             )
 
-        nc.scalar.copy(out=woven(a_bf[0][:]), in_=planar(a_raw[0][:]))
-        h = sb.tile([P, PACK, S], F32, name="h", tag="first", align_bytes=64)
-        for t in range(PACK):
-            nc.scalar.activation(out=h[:, t, :], in_=h_bank[t][:], func=ACT.Silu)
-        for d, t in [(d, t) for d in range(2) for t in range(PACK)]:
-            nc.scalar.activation(func=ACT.Copy, **fetch_args(h, d, t))
-
-        deal(nc.vector.tensor_copy, w3_bf, w3_raw[0], 0)
-        quantize(a_mx[0], a_bf[0][:])
-        deal(nc.vector.tensor_copy, w3_bf, w3_raw[1], HALF // PACK)
-        quantize(w3_mx, w3_bf[:])
-        filters(0)
-        a_bf.append(sb.tile([P, PACK * V], BF16, name="a_bf1", tag="chain", align_bytes=64))
-        nc.vector.tensor_copy(out=woven(a_bf[1][:]), in_=planar(a_raw[1][:]))
-        term.append(sb.tile([P, PACK, V], F32, name="term0", tag="second", align_bytes=64))
-        quantize(a_mx[1], a_bf[1][:])
-        filters(1)
-        weigh(0, 0)
-        w2_bf = sb.tile([P, PACK * H], BF16, name="w2_bf", tag="chain", align_bytes=64)
-        deal(nc.vector.tensor_copy, w2_bf, w2_raw, 0)
-        weigh(0, 1)
-        quantize(w2_mx, w2_bf[:])
-        term.append(sb.tile([P, PACK, V], F32, name="term1", tag="chain", align_bytes=64))
         z_bf = [sb.tile([P, PACK * VH], BF16, name=f"z_bf{part}", align_bytes=64) for part in range(2)]
         z_mx = [mx_tiles(VH, f"z{part}") for part in range(2)]
         part_cols = [slice(part * VH, (part + 1) * VH) for part in range(2)]
@@ -185,8 +178,8 @@ def tile_picked_dime_none_lo_kernel(
         def keep(part, pair):
             nc.scalar.copy(out=y[part][:, 2 * pair : 2 * pair + 2, :], in_=y_bank[part][pair][:])
 
-        def round_pair(part, pair):
-            nc.vector.tensor_copy(
+        def round_pair(copy, part, pair):
+            copy(
                 out=y_bf[part][:].rearrange("p (c j) -> p c j", j=PACK)[:, :, 2 * pair : 2 * pair + 2],
                 in_=y_bank[part][pair][:].rearrange("p j c -> p c j"),
             )
@@ -194,30 +187,37 @@ def tile_picked_dime_none_lo_kernel(
         def store_y(part):
             nc.sync.dma_start(out=by_rows(out_0)[:, :, part_cols[part]], in_=y[part][:])
 
-        weigh(1, 0, part_cols[0])
-        weigh(1, 1, part_cols[0])
-        weigh(1, 0, part_cols[1])
+        def store_words(part):
+            words = out_1[0].rearrange("p c r -> p (c r)").bitcast(I32)
+            nc.sync.dma_start(out=words[:, part_cols[part]], in_=y_mx[0][:, part_cols[part]].bitcast(I32))
+
+        weigh(0, 0)
+        weigh(0, 1)
+        weigh(1, 0)
+        weigh(1, 1)
         add_terms(0)
-        weigh(1, 1, part_cols[1])
+        w2_mx = mx_tiles(H, "w2", "picked11")
+        quantize(w2_mx, w2_bf[:])
         quantize(z_mx[0], z_bf[0][:])
         project(0)
         add_terms(1)
         quantize(z_mx[1], z_bf[1][:])
         project(1)
 
-        keep(0, 0)
-        keep(0, 1)
+        for pair in range(2):
+            round_pair(nc.vector.tensor_copy, 0, pair)
+            keep(0, pair)
         store_y(0)
-        nc.vector.tensor_copy(out=woven(y_bf[0][:]), in_=planar(y[0][:]))
-        round_pair(1, 0)
+        round_pair(nc.vector.tensor_copy, 1, 0)
         keep(1, 1)
         keep(1, 0)
         store_y(1)
         quantize(y_mx, y_bf[0][:], part_cols[0])
-        round_pair(1, 1)
+        store_words(0)
+        round_pair(nc.vector.tensor_copy, 1, 1)
         quantize(y_mx, y_bf[1][:], part_cols[1])
+        store_words(1)
 
-        nc.sync.dma_start(out=out_1[0].rearrange("p c r -> p (c r)").bitcast(I32), in_=y_mx[0][:].bitcast(I32))
         for q in range(4):
             queue = nc.scalar if q % 2 else nc.sync
             queue.dma_start(

@@ -18,7 +18,7 @@ ALU = mybir.AluOpType
 P = 128
 PACK = 4
 VH = 128
-W1_SCALAR = 48
+W1_SCALAR = 56
 
 
 def tile_picked_dime_none_lo_kernel(
@@ -93,10 +93,15 @@ def tile_picked_dime_none_lo_kernel(
         nc.scalar.activation(out=warm[:, 1:2], in_=warm[:, 0:1], func=ACT.Silu)
 
         x_bf = sb.tile([P, S, PACK], BF16, name="x_bf", align_bytes=64)
-        for j in range(PACK):
+        for j in range(PACK - 1):
             nc.vector.tensor_copy(out=x_bf[:, :, j], in_=x_raw[j][:].indirect(offs_sb[:]))
         x_mx = mx_tiles(S, "x")
-        quantize(x_mx, x_bf[:].rearrange("p s j -> p (s j)"))
+        halves = [slice(half * S // 2, (half + 1) * S // 2) for half in range(2)]
+        for cols in halves:
+            entries = offs_sb[:, cols.start // 16 : cols.stop // 16]
+            nc.vector.tensor_copy(out=x_bf[:, cols, PACK - 1], in_=x_raw[PACK - 1][:].indirect(entries))
+        for cols in halves:
+            quantize(x_mx, x_bf[:, cols, :].rearrange("p s j -> p (s j)"), cols)
 
         w1_bf = sb.tile([P, PACK * H], BF16, name="w1_bf", align_bytes=64)
         deal(nc.scalar.copy, w1_bf, w1_raw[:, :, : PACK * W1_SCALAR], 0, W1_SCALAR)
@@ -117,7 +122,7 @@ def tile_picked_dime_none_lo_kernel(
 
         picked = [
             [
-                sb.tile([P, 2, V], F32, name=f"picked{d}{pair}", tag=f"picked{d}{pair}", align_bytes=64)
+                sb.tile([P, 2, V], F32, name=f"picked{d}{pair}", tag="w3_raw" if d + pair == 0 else f"picked{d}{pair}", align_bytes=64)
                 for pair in range(2)
             ]
             for d in range(2)
@@ -126,8 +131,9 @@ def tile_picked_dime_none_lo_kernel(
         def fetch_args(d, t):
             return {"out": picked[d][t // 2][:, t % 2, :], "in_": h[t][:].indirect(pos_sb[d][:])}
 
+        nc.vector.tensor_copy(**fetch_args(0, 0))
         quantize(w3_mx, w3_bf[:])
-        for d, t in [(d, t) for d in range(2) for t in range(PACK)]:
+        for d, t in [(d, t) for d in range(2) for t in range(PACK)][1:]:
             nc.scalar.activation(func=ACT.Copy, **fetch_args(d, t))
 
         a_bf = [sb.tile([P, PACK * V], BF16, name=f"a_bf{d}", align_bytes=64) for d in range(2)]
@@ -148,9 +154,12 @@ def tile_picked_dime_none_lo_kernel(
         deal(nc.scalar.copy, w2_bf, w2_raw[1][:], P // 2, P)
         term = [sb.tile([P, PACK, V], F32, name=f"term{d}", tag="term1" if d else "w2_raw0") for d in range(2)]
 
-        def weigh(d, pair):
+        def weigh(d, pair, cols=slice(None)):
             nc.vector.tensor_tensor(
-                out=term[d][:, 2 * pair : 2 * pair + 2, :], in0=picked[d][pair][:], in1=f_bank[d][pair][:], op=ALU.mult
+                out=term[d][:, 2 * pair : 2 * pair + 2, cols],
+                in0=picked[d][pair][:, :, cols],
+                in1=f_bank[d][pair][:, :, cols],
+                op=ALU.mult,
             )
 
         z_bf = [sb.tile([P, PACK * VH], BF16, name=f"z_bf{part}", align_bytes=64) for part in range(2)]
@@ -178,12 +187,6 @@ def tile_picked_dime_none_lo_kernel(
         def keep(part, pair):
             nc.scalar.copy(out=y[part][:, 2 * pair : 2 * pair + 2, :], in_=y_bank[part][pair][:])
 
-        def round_pair(copy, part, pair):
-            copy(
-                out=y_bf[part][:].rearrange("p (c j) -> p c j", j=PACK)[:, :, 2 * pair : 2 * pair + 2],
-                in_=y_bank[part][pair][:].rearrange("p j c -> p c j"),
-            )
-
         def store_y(part):
             nc.sync.dma_start(out=by_rows(out_0)[:, :, part_cols[part]], in_=y[part][:])
 
@@ -194,7 +197,8 @@ def tile_picked_dime_none_lo_kernel(
         weigh(0, 0)
         weigh(0, 1)
         weigh(1, 0)
-        weigh(1, 1)
+        weigh(1, 1, part_cols[0])
+        weigh(1, 1, part_cols[1])
         add_terms(0)
         w2_mx = mx_tiles(H, "w2", "picked11")
         quantize(w2_mx, w2_bf[:])
@@ -204,19 +208,13 @@ def tile_picked_dime_none_lo_kernel(
         quantize(z_mx[1], z_bf[1][:])
         project(1)
 
-        for pair in range(2):
-            round_pair(nc.vector.tensor_copy, 0, pair)
-            keep(0, pair)
-        store_y(0)
-        round_pair(nc.vector.tensor_copy, 1, 0)
-        keep(1, 1)
-        keep(1, 0)
-        store_y(1)
-        quantize(y_mx, y_bf[0][:], part_cols[0])
-        store_words(0)
-        round_pair(nc.vector.tensor_copy, 1, 1)
-        quantize(y_mx, y_bf[1][:], part_cols[1])
-        store_words(1)
+        for part in range(2):
+            keep(part, 0)
+            keep(part, 1)
+            store_y(part)
+            nc.vector.tensor_copy(out=woven(y_bf[part][:]), in_=planar(y[part][:]))
+            quantize(y_mx, y_bf[part][:], part_cols[part])
+            store_words(part)
 
         for q in range(4):
             queue = nc.scalar if q % 2 else nc.sync

from contextlib import ExitStack

import concourse.mybir as mybir

K, T, S, V, H = 512, 2048, 512, 256, 512
FLOPS = 2 * (K * H * S + K * H * 2 * V + H * H * V)

F32 = mybir.dt.float32
BF16 = mybir.dt.bfloat16
I32 = mybir.dt.int32
U32 = mybir.dt.uint32
U16 = mybir.dt.uint16
U8 = mybir.dt.uint8
FP8X4 = mybir.dt.float8_e4m3fn_x4
ACT = mybir.ActivationFunctionType
ALU = mybir.AluOpType

P = 128
PACK = 4
VH = 128
W1_SCALAR = 56


def tile_picked_dime_none_lo_kernel(
    tc, xT, aT, w1, w3, w2, offs, pos1, pos2, out_0, out_1, out_2
):
    nc = tc.nc
    with ExitStack() as ctx:
        lists = ctx.enter_context(tc.tile_pool(name="lists", bufs=1))
        sb = ctx.enter_context(tc.tile_pool(name="sb", bufs=1))
        psum = ctx.enter_context(tc.psum_pool(name="psum", bufs=1))

        def by_rows(dram):
            return dram.rearrange("(p j) c -> p j c", j=PACK)

        def load(dram, name):
            raw = sb.tile([P, PACK, H], F32, name=name, tag=name, align_bytes=64)
            nc.sync.dma_start(out=raw[:], in_=by_rows(dram))
            return raw

        def mx_tiles(width, name, tag=None):
            codes = sb.tile([P, width], U32, name=name + "_codes", tag=tag or name + "_codes", align_bytes=64)
            scales = sb.tile([P, width], U8, name=name + "_scales", align_bytes=64)
            return codes, scales

        def quantize(mx, rounded, cols=slice(None)):
            codes, scales = mx
            nc.vector.quantize_mx(out=codes[:, cols].bitcast(FP8X4), scales=scales[:, cols], in_=rounded)

        def product(out, weights, t, moving):
            cols = slice(t * P, (t + 1) * P)
            nc.tensor.matmul_mx(
                out=out,
                lhsT=weights[0][:, cols].bitcast(FP8X4),
                lhsT_scale=weights[1][:, cols],
                rhs=moving[0][:].bitcast(FP8X4),
                rhs_scale=moving[1][:],
                start=True,
                stop=True,
            )

        def deal(copy, rounded, raw, m0, m1):
            copy(
                out=rounded[:].rearrange("p (t m j) -> p m j t", t=PACK, j=PACK)[:, m0:m1],
                in_=raw.rearrange("p j (m t) -> p m j t", t=PACK),
            )

        def woven(ap):
            return ap.rearrange("p (c i j) -> p c j i", i=4, j=PACK)

        def planar(ap):
            return ap.rearrange("p j (c i) -> p c j i", i=4)

        offs_sb = lists.tile([P, S // 16], U16, name="offs_sb")
        pos_sb = [lists.tile([P, V // 16], U16, name=f"pos{d}_sb") for d in range(2)]

        x_raw = [sb.tile([P, T], F32, name=f"x_raw{j}") for j in range(PACK)]
        nc.sync.dma_start(out=x_raw[0][:], in_=by_rows(xT)[:, 0, :])
        nc.sync.dma_start(offs_sb[:], offs)
        for j in range(1, PACK):
            nc.sync.dma_start(out=x_raw[j][:], in_=by_rows(xT)[:, j, :])
        w1_raw = load(w1, "w1_raw")
        nc.sync.dma_start(pos_sb[0][:], pos1)
        nc.sync.dma_start(pos_sb[1][:], pos2)
        w3_raw = load(w3, "w3_raw")
        a_raw = load(aT, "a_raw")
        w2_raw = [sb.tile([P, PACK, H // 2], F32, name=f"w2_raw{half}", tag=f"w2_raw{half}") for half in range(2)]
        for half in range(2):
            nc.sync.dma_start(out=w2_raw[half][:], in_=by_rows(w2)[:, :, half * H // 2 : (half + 1) * H // 2])

        warm = sb.tile([P, 2], F32, name="warm")
        nc.vector.memset(warm[:, 0:1], 0.0)
        nc.scalar.activation(out=warm[:, 1:2], in_=warm[:, 0:1], func=ACT.Silu)

        x_bf = sb.tile([P, S, PACK], BF16, name="x_bf", align_bytes=64)
        for j in range(PACK - 1):
            nc.vector.tensor_copy(out=x_bf[:, :, j], in_=x_raw[j][:].indirect(offs_sb[:]))
        x_mx = mx_tiles(S, "x")
        halves = [slice(half * S // 2, (half + 1) * S // 2) for half in range(2)]
        for cols in halves:
            entries = offs_sb[:, cols.start // 16 : cols.stop // 16]
            nc.vector.tensor_copy(out=x_bf[:, cols, PACK - 1], in_=x_raw[PACK - 1][:].indirect(entries))
        for cols in halves:
            quantize(x_mx, x_bf[:, cols, :].rearrange("p s j -> p (s j)"), cols)

        w1_bf = sb.tile([P, PACK * H], BF16, name="w1_bf", align_bytes=64)
        deal(nc.scalar.copy, w1_bf, w1_raw[:, :, : PACK * W1_SCALAR], 0, W1_SCALAR)
        deal(nc.vector.tensor_copy, w1_bf, w1_raw[:, :, PACK * W1_SCALAR :], W1_SCALAR, P)
        w1_mx = mx_tiles(H, "w1")
        quantize(w1_mx, w1_bf[:, : PACK * P], slice(0, P))
        quantize(w1_mx, w1_bf[:, PACK * P :], slice(P, H))

        h_bank = [psum.tile([P, S], F32, name=f"h_bank{t}", tag=f"bank{t}") for t in range(PACK)]
        h = [sb.tile([P, S], F32, name=f"h{t}") for t in range(PACK)]
        for t in range(PACK):
            product(h_bank[t][:], w1_mx, t, x_mx)
            nc.scalar.activation(out=h[t][:], in_=h_bank[t][:], func=ACT.Silu)

        w3_bf = sb.tile([P, PACK * H], BF16, name="w3_bf", align_bytes=64)
        w3_mx = mx_tiles(H, "w3")
        deal(nc.vector.tensor_copy, w3_bf, w3_raw[:], 0, P)

        picked = [
            [
                sb.tile([P, 2, V], F32, name=f"picked{d}{pair}", tag="w3_raw" if d + pair == 0 else f"picked{d}{pair}", align_bytes=64)
                for pair in range(2)
            ]
            for d in range(2)
        ]

        def fetch_args(d, t):
            return {"out": picked[d][t // 2][:, t % 2, :], "in_": h[t][:].indirect(pos_sb[d][:])}

        nc.vector.tensor_copy(**fetch_args(0, 0))
        quantize(w3_mx, w3_bf[:])
        for d, t in [(d, t) for d in range(2) for t in range(PACK)][1:]:
            nc.scalar.activation(func=ACT.Copy, **fetch_args(d, t))

        a_bf = [sb.tile([P, PACK * V], BF16, name=f"a_bf{d}", align_bytes=64) for d in range(2)]
        a_mx = [mx_tiles(V, f"a{d}") for d in range(2)]
        f_bank = [
            [psum.tile([P, 2, V], F32, name=f"f_bank{d}{pair}", tag=f"bank{4 + 2 * d + pair}") for pair in range(2)]
            for d in range(2)
        ]
        for d in range(2):
            nc.vector.tensor_copy(out=woven(a_bf[d][:]), in_=planar(a_raw[:, :, d * V : (d + 1) * V]))
        for d in range(2):
            quantize(a_mx[d], a_bf[d][:])
            for t in range(PACK):
                product(f_bank[d][t // 2][:, t % 2, :], w3_mx, t, a_mx[d])

        w2_bf = sb.tile([P, PACK * H], BF16, name="w2_bf", align_bytes=64)
        deal(nc.vector.tensor_copy, w2_bf, w2_raw[0][:], 0, P // 2)
        deal(nc.scalar.copy, w2_bf, w2_raw[1][:], P // 2, P)
        term = [sb.tile([P, PACK, V], F32, name=f"term{d}", tag="term1" if d else "w2_raw0") for d in range(2)]

        def weigh(d, pair, cols=slice(None)):
            nc.vector.tensor_tensor(
                out=term[d][:, 2 * pair : 2 * pair + 2, cols],
                in0=picked[d][pair][:, :, cols],
                in1=f_bank[d][pair][:, :, cols],
                op=ALU.mult,
            )

        z_bf = [sb.tile([P, PACK * VH], BF16, name=f"z_bf{part}", align_bytes=64) for part in range(2)]
        z_mx = [mx_tiles(VH, f"z{part}") for part in range(2)]
        part_cols = [slice(part * VH, (part + 1) * VH) for part in range(2)]

        def add_terms(part):
            cols = part_cols[part]
            nc.vector.tensor_tensor(
                out=woven(z_bf[part][:]), in0=planar(term[0][:, :, cols]), in1=planar(term[1][:, :, cols]), op=ALU.add
            )

        y_bank = [
            [psum.tile([P, 2, VH], F32, name=f"y_bank{part}{pair}", tag=f"bank{2 * part + pair}") for pair in range(2)]
            for part in range(2)
        ]
        y = [sb.tile([P, PACK, VH], F32, name=f"y{part}") for part in range(2)]
        y_bf = [sb.tile([P, PACK * VH], BF16, name=f"y_bf{part}", align_bytes=64) for part in range(2)]
        y_mx = mx_tiles(V, "y")

        def project(part):
            for t in range(PACK):
                product(y_bank[part][t // 2][:, t % 2, :], w2_mx, t, z_mx[part])

        def keep(part, pair):
            nc.scalar.copy(out=y[part][:, 2 * pair : 2 * pair + 2, :], in_=y_bank[part][pair][:])

        def store_y(part):
            nc.sync.dma_start(out=by_rows(out_0)[:, :, part_cols[part]], in_=y[part][:])

        def store_words(part):
            words = out_1[0].rearrange("p c r -> p (c r)").bitcast(I32)
            nc.sync.dma_start(out=words[:, part_cols[part]], in_=y_mx[0][:, part_cols[part]].bitcast(I32))

        weigh(0, 0)
        weigh(0, 1)
        weigh(1, 0)
        weigh(1, 1, part_cols[0])
        weigh(1, 1, part_cols[1])
        add_terms(0)
        w2_mx = mx_tiles(H, "w2", "picked11")
        quantize(w2_mx, w2_bf[:])
        quantize(z_mx[0], z_bf[0][:])
        project(0)
        add_terms(1)
        quantize(z_mx[1], z_bf[1][:])
        project(1)

        for part in range(2):
            keep(part, 0)
            keep(part, 1)
            store_y(part)
            nc.vector.tensor_copy(out=woven(y_bf[part][:]), in_=planar(y[part][:]))
            quantize(y_mx, y_bf[part][:], part_cols[part])
            store_words(part)

        for q in range(4):
            queue = nc.scalar if q % 2 else nc.sync
            queue.dma_start(
                out=out_2[0][4 * q : 4 * q + 4, :].bitcast(I32), in_=y_mx[1][32 * q : 32 * q + 4, :].bitcast(I32)
            )
